import numpy as np
import ml_dtypes


def mxq(x, axis, fmt="e4m3"):
    dtype, down = {"e4m3": (ml_dtypes.float8_e4m3fn, 7), "e5m2": (ml_dtypes.float8_e5m2, 14)}[fmt]
    v = np.moveaxis(np.asarray(x, np.float32).astype(ml_dtypes.bfloat16).astype(np.float64), axis, -1)
    blocks = v.reshape(v.shape[:-1] + (-1, 32))
    amax = np.abs(blocks).max(-1, keepdims=True)
    byte = np.maximum(np.where(amax > 0, np.frexp(amax)[1] - 1 + 127, 0) - down, 1)
    scale = np.exp2(byte - 127.0)
    codes = (blocks / scale).astype(np.float32).astype(dtype).astype(np.float64)
    return np.moveaxis((codes * scale).reshape(v.shape), -1, axis)


WIDE = False


def mx_kscale(k):
    if not WIDE:
        return np.ones(k)
    levels = np.array([10, -10, 5, -5, 0])
    if k % 512:
        return np.exp2(np.random.permutation(np.resize(levels, k // 32))).repeat(32)
    a = np.empty((k // 512, 16))
    for p in range(k // 512):
        a[p, :8] = np.random.permutation(np.resize(levels, 8))
        for g in range(8):
            far = levels[np.abs(levels - a[p, g]) >= 10]
            a[p, g + 8] = far[np.random.randint(len(far))]
    return np.exp2(a.ravel()).repeat(32)


def f64(x):
    return np.asarray(x).astype(np.float64)


def striped(idx):
    return np.tile(np.asarray(idx).reshape(-1, 16).T, (8, 1)).astype(np.uint16)


def unstriped(offs):
    return offs[:16].T.reshape(-1).astype(np.int64)


E2M1 = np.array([0.0, 0.5, 1.0, 1.5, 2.0, 3.0, 4.0, 6.0, -0.0, -0.5, -1.0, -1.5, -2.0, -3.0, -4.0, -6.0])


def pack_weight(w, fmt):
    k, n = w.shape
    w = f64(np.asarray(w, np.float32).astype(ml_dtypes.bfloat16)).reshape(k // 32, 32, n)
    amax = np.abs(w).max(1)
    if fmt == "e4m3":
        byte = np.frexp(amax)[1] - 1 + 127 - 7
    else:
        mant, ex = np.frexp(amax / 6.0)
        byte = np.where(mant > 0.5, ex, ex - 1) + 127
    byte = np.clip(np.where(amax > 0, byte, 1), 1, 254)
    scaled = (w * np.exp2(127.0 - byte)[:, None, :]).reshape(k, n).astype(np.float32)
    by_word = np.ascontiguousarray(scaled.reshape(k // 512, 128, 4, n).transpose(0, 1, 3, 2))
    if fmt == "e4m3":
        words = by_word.astype(ml_dtypes.float8_e4m3fn).view(np.uint8)
    else:
        c = by_word.astype(ml_dtypes.float4_e2m1fn).view(np.uint8) & 0xF
        words = (c[..., 0::2] | (c[..., 1::2] << 4)).reshape(k // 512, 128, 2 * n)
    return np.ascontiguousarray(words), np.ascontiguousarray(byte.astype(np.uint8).reshape(k // 512, 16, n))


def unpack_weight(words, scales, fmt):
    g, _, n = scales.shape
    words = np.ascontiguousarray(words).reshape(g, 128, n, -1)
    if fmt == "e4m3":
        vals = words.view(ml_dtypes.float8_e4m3fn).astype(np.float64)
    else:
        nib = np.empty((g, 128, n, 4), np.uint8)
        nib[..., 0::2] = words & 0xF
        nib[..., 1::2] = words >> 4
        vals = E2M1[nib]
    vals = vals * np.repeat(np.exp2(scales.astype(np.float64) - 127.0), 8, axis=1)[..., None]
    return vals.transpose(0, 1, 3, 2).reshape(g * 512, n)


K, T, J, N = 512, 2048, 512, 256


def setup_inputs():
    n = np.random.standard_normal
    idx = np.random.permutation(T)[:J]
    fk = mx_kscale(K)
    xqp = pack_weight(n((K, T)) / fk[:, None], "e2m1")
    wp = pack_weight(n((K, N)) * 1 / np.sqrt(K) * fk[:, None], "e4m3")
    wep = pack_weight(n((K, N)) * 1 / np.sqrt(K) * fk[:, None], "e2m1")
    return {
        "xq_words": xqp[0],
        "xq_scales": xqp[1],
        "w_words": wp[0],
        "w_scales": wp[1],
        "xf": (n((K, T)) / fk[:, None]).astype(np.float32),
        "xc": (n((K, T)) * 0.9 / fk[:, None]).astype(np.float32),
        "we_words": wep[0],
        "we_scales": wep[1],
        "offs": striped(idx),
    }


def reference(xq_words, xq_scales, w_words, w_scales, xf, xc, we_words, we_scales, offs):
    idx = unstriped(offs)
    xqu = unpack_weight(xq_words, xq_scales, "e2m1")
    wu = unpack_weight(w_words, w_scales, "e4m3")
    weu = unpack_weight(we_words, we_scales, "e2m1")
    z = wu.T @ xqu
    e = f64(xf)[:, idx] - f64(xc)[:, idx]
    eq = mxq(e, 0, "e4m3")
    p = weu.T @ eq
    d = np.tanh(p)
    dp = np.zeros((N, T))
    dp[:, idx] = d
    y = z + dp
    return y

@@ -1,0 +1,153 @@
+from contextlib import ExitStack
+
+import concourse.mybir as mybir
+
+K, T, J, N = 512, 2048, 512, 256
+FLOPS = 2 * K * N * (T + J)
+
+F32 = mybir.dt.float32
+BF16 = mybir.dt.bfloat16
+I32 = mybir.dt.int32
+U32 = mybir.dt.uint32
+U16 = mybir.dt.uint16
+U8 = mybir.dt.uint8
+FP8X4 = mybir.dt.float8_e4m3fn_x4
+FP4X4 = mybir.dt.float4_e2m1fn_x4
+SUB = mybir.AluOpType.subtract
+ADD = mybir.AluOpType.add
+TANH = mybir.ActivationFunctionType.Tanh
+
+P = 128
+PACK = 4
+CH = 128
+NCH = J // CH
+BANK = 512
+
+
+def load_scales(queue, plane, rows):
+    for q in range(4):
+        queue.dma_start(out=plane[32 * q : 32 * q + 4, :].bitcast(I32), in_=rows[0, 4 * q : 4 * q + 4, :].bitcast(I32))
+
+
+def tile_list_error_feedback_lists_kernel(tc, xq_words, xq_scales, w_words, w_scales, xf, xc, we_words, we_scales, offs, out):
+    nc = tc.nc
+    with ExitStack() as ctx:
+        keep = ctx.enter_context(tc.tile_pool(name="keep", bufs=1))
+        psum = ctx.enter_context(tc.psum_pool(name="psum", bufs=1))
+
+        offsets = keep.tile([P, J // 16], U16, name="offsets")
+        nc.sync.dma_start(offsets[:], offs)
+
+        xc_rows = xc.rearrange("(p t) c -> p (t c)", t=PACK)
+        xf_rows = xf.rearrange("(p t) c -> p (t c)", t=PACK)
+        xc01 = keep.tile([P, 2 * T], F32, name="xc01")
+        xc2 = keep.tile([P, T], F32, name="xc2")
+        xc3 = keep.tile([P, T], F32, name="xc3")
+        xf_t = [keep.tile([P, T], F32, name="xf%d" % t) for t in range(PACK)]
+        nc.sync.dma_start(out=xc01[:], in_=xc_rows[:, 0 : 2 * T])
+        nc.sync.dma_start(out=xf_t[0][:], in_=xf_rows[:, 0:T])
+        nc.sync.dma_start(out=xf_t[1][:], in_=xf_rows[:, T : 2 * T])
+        nc.sync.dma_start(out=xc2[:], in_=xc_rows[:, 2 * T : 3 * T])
+        nc.sync.dma_start(out=xf_t[2][:], in_=xf_rows[:, 2 * T : 3 * T])
+        nc.sync.dma_start(out=xc3[:], in_=xc_rows[:, 3 * T : 4 * T])
+        nc.sync.dma_start(out=xf_t[3][:], in_=xf_rows[:, 3 * T : 4 * T])
+        xc_win = [xc01[:, 0:T], xc01[:, T : 2 * T], xc2[:], xc3[:]]
+
+        we_sc = keep.tile([P, N], U8, name="we_sc", align_bytes=64)
+        w_sc = keep.tile([P, N], U8, name="w_sc", align_bytes=64)
+        xq_sc = keep.tile([P, T], U8, name="xq_sc", align_bytes=64)
+        for plane in (we_sc, w_sc, xq_sc):
+            nc.vector.memset(plane[:].bitcast(I32), 0)
+        load_scales(nc.gpsimd, w_sc, w_scales)
+
+        we_w = keep.tile([P, 2 * N], U8, name="we_w", align_bytes=64)
+        xq_w = keep.tile([P, 2 * T], U8, name="xq_w", align_bytes=64)
+        w_w = keep.tile([P, N], U32, name="w_w", align_bytes=64)
+        nc.sync.dma_start(out=we_w[:].bitcast(I32), in_=we_words[0].bitcast(I32))
+        load_scales(nc.sync, we_sc, we_scales)
+        nc.sync.dma_start(out=xq_w[:].bitcast(I32), in_=xq_words[0].bitcast(I32))
+        nc.sync.dma_start(out=w_w[:].bitcast(I32), in_=w_words[0].rearrange("p n t -> p (n t)").bitcast(I32))
+        load_scales(nc.sync, xq_sc, xq_scales)
+
+        dp = keep.tile([P, T], F32, name="dp")
+        nc.vector.memset(dp[:], 0.0)
+
+        woven = [keep.tile([P, CH, PACK], BF16, name="woven%d" % c, align_bytes=64) for c in range(NCH)]
+        picked = [keep.tile([P, J], F32, name="picked%d" % t) for t in range(PACK)]
+        for t in range(PACK - 1):
+            nc.vector.tensor_copy(picked[t][:], xc_win[t].indirect(offsets[:]))
+            e = keep.tile([P, J], F32, name="e%d" % t)
+            nc.vector.tensor_tensor(e[:], xf_t[t][:].indirect(offsets[:]), picked[t][:], SUB)
+            for c in range(NCH):
+                nc.scalar.copy(out=woven[c][:, :, t], in_=e[:, c * CH : (c + 1) * CH])
+        last = PACK - 1
+        nc.vector.tensor_copy(picked[last][:], xc_win[last].indirect(offsets[:]))
+
+        codes = [keep.tile([P, CH], U32, name="codes%d" % c, align_bytes=64) for c in range(NCH)]
+        scales = [keep.tile([P, CH], U8, name="scales%d" % c, align_bytes=64) for c in range(NCH)]
+
+        def gather_last(c):
+            e = keep.tile([P, CH], F32, name="elast%d" % c)
+            cols = slice(c * CH // 16, (c + 1) * CH // 16)
+            nc.vector.tensor_tensor(e[:], xf_t[last][:].indirect(offsets[:, cols]), picked[last][:, c * CH : (c + 1) * CH], SUB)
+            nc.scalar.copy(out=woven[c][:, :, last], in_=e[:])
+
+        def product(c, h):
+            p = psum.tile([P, CH], F32, name="p%d_%d" % (h, c), tag="bank%d" % (4 * h + c))
+            nc.tensor.matmul_mx(
+                out=p[:],
+                lhsT=we_w[:, 2 * P * h : 2 * P * (h + 1)].bitcast(FP4X4),
+                lhsT_scale=we_sc[:, P * h : P * (h + 1)],
+                rhs=codes[c][:].bitcast(FP8X4),
+                rhs_scale=scales[c][:],
+                start=True,
+                stop=True,
+            )
+            return p
+
+        def quantise(c):
+            nc.vector.quantize_mx(out=codes[c][:].bitcast(FP8X4), scales=scales[c][:], in_=woven[c][:].rearrange("p j t -> p (j t)"))
+            p0 = product(c, 0)
+            p1.append(product(c, 1))
+            nc.scalar.activation(d0[c // 2][:, (c % 2) * CH : (c % 2 + 1) * CH], p0[:], TANH)
+
+        d0 = [keep.tile([P, 2 * CH], F32, name="d0_%d" % i) for i in range(2)]
+        d1 = keep.tile([P, J], F32, name="d1")
+        p1 = []
+        gather_last(0)
+        gather_last(1)
+        gather_last(2)
+        quantise(0)
+        gather_last(3)
+        quantise(1)
+        quantise(2)
+        quantise(3)
+        for c in range(NCH):
+            nc.scalar.activation(d1[:, c * CH : (c + 1) * CH], p1[c][:], TANH)
+
+        def dense(h, b):
+            z = psum.tile([P, BANK], F32, name="z%d_%d" % (h, b), tag="bank%d" % (4 * h + b))
+            nc.tensor.matmul_mx(
+                out=z[:],
+                lhsT=w_w[:, P * h : P * (h + 1)].bitcast(FP8X4),
+                lhsT_scale=w_sc[:, P * h : P * (h + 1)],
+                rhs=xq_w[:, 2 * BANK * b : 2 * BANK * (b + 1)].bitcast(FP4X4),
+                rhs_scale=xq_sc[:, BANK * b : BANK * (b + 1)],
+                start=True,
+                stop=True,
+            )
+            return z
+
+        def finish(h, zs):
+            for b in range(T // BANK):
+                o = keep.tile([P, BANK], F32, name="o%d_%d" % (h, b))
+                nc.vector.tensor_tensor(o[:], zs[b][:], dp[:, BANK * b : BANK * (b + 1)], ADD)
+                nc.sync.dma_start(out=out[P * h : P * (h + 1), BANK * b : BANK * (b + 1)], in_=o[:])
+
+        z0 = [dense(0, b) for b in range(T // BANK)]
+        z1 = [dense(1, b) for b in range(T // BANK)]
+        for i in range(2):
+            nc.vector.tensor_copy(dp[:].indirect(offsets[:, 16 * i : 16 * (i + 1)]), d0[i][:])
+        finish(0, z0)
+        nc.vector.tensor_copy(dp[:].indirect(offsets[:]), d1[:])
+        finish(1, z1)

@@ -1,6 +1,7 @@
 from contextlib import ExitStack
 
 import concourse.mybir as mybir
+from concourse.masks import make_identity
 
 K, T, J, N = 512, 2048, 512, 256
 FLOPS = 2 * K * N * (T + J)
@@ -36,7 +37,6 @@ def tile_list_error_feedback_lists_kernel(tc, xq_words, xq_scales, w_words, w_sc
         psum = ctx.enter_context(tc.psum_pool(name="psum", bufs=1))
 
         offsets = keep.tile([P, J // 16], U16, name="offsets")
-        nc.sync.dma_start(offsets[:], offs)
 
         xc_rows = xc.rearrange("(p t) c -> p (t c)", t=PACK)
         xf_rows = xf.rearrange("(p t) c -> p (t c)", t=PACK)
@@ -45,6 +45,7 @@ def tile_list_error_feedback_lists_kernel(tc, xq_words, xq_scales, w_words, w_sc
         xc3 = keep.tile([P, T], F32, name="xc3")
         xf_t = [keep.tile([P, T], F32, name="xf%d" % t) for t in range(PACK)]
         nc.sync.dma_start(out=xc01[:], in_=xc_rows[:, 0 : 2 * T])
+        nc.sync.dma_start(offsets[:], offs)
         nc.sync.dma_start(out=xf_t[0][:], in_=xf_rows[:, 0:T])
         nc.sync.dma_start(out=xf_t[1][:], in_=xf_rows[:, T : 2 * T])
         nc.sync.dma_start(out=xc2[:], in_=xc_rows[:, 2 * T : 3 * T])
@@ -58,19 +59,22 @@ def tile_list_error_feedback_lists_kernel(tc, xq_words, xq_scales, w_words, w_sc
         xq_sc = keep.tile([P, T], U8, name="xq_sc", align_bytes=64)
         for plane in (we_sc, w_sc, xq_sc):
             nc.vector.memset(plane[:].bitcast(I32), 0)
+        ident = keep.tile([P, P], F32, name="ident")
+        make_identity(nc, ident[:])
+        load_scales(nc.gpsimd, we_sc, we_scales)
         load_scales(nc.gpsimd, w_sc, w_scales)
 
         we_w = keep.tile([P, 2 * N], U8, name="we_w", align_bytes=64)
         xq_w = keep.tile([P, 2 * T], U8, name="xq_w", align_bytes=64)
         w_w = keep.tile([P, N], U32, name="w_w", align_bytes=64)
         nc.sync.dma_start(out=we_w[:].bitcast(I32), in_=we_words[0].bitcast(I32))
-        load_scales(nc.sync, we_sc, we_scales)
         nc.sync.dma_start(out=xq_w[:].bitcast(I32), in_=xq_words[0].bitcast(I32))
         nc.sync.dma_start(out=w_w[:].bitcast(I32), in_=w_words[0].rearrange("p n t -> p (n t)").bitcast(I32))
         load_scales(nc.sync, xq_sc, xq_scales)
 
-        dp = keep.tile([P, T], F32, name="dp")
-        nc.vector.memset(dp[:], 0.0)
+        dp = [keep.tile([P, T], F32, name="dp%d" % h) for h in range(2)]
+        for h in range(2):
+            nc.vector.memset(dp[h][:], 0.0)
 
         woven = [keep.tile([P, CH, PACK], BF16, name="woven%d" % c, align_bytes=64) for c in range(NCH)]
         picked = [keep.tile([P, J], F32, name="picked%d" % t) for t in range(PACK)]
@@ -138,16 +142,44 @@ def tile_list_error_feedback_lists_kernel(tc, xq_words, xq_scales, w_words, w_sc
             )
             return z
 
-        def finish(h, zs):
-            for b in range(T // BANK):
-                o = keep.tile([P, BANK], F32, name="o%d_%d" % (h, b))
-                nc.vector.tensor_tensor(o[:], zs[b][:], dp[:, BANK * b : BANK * (b + 1)], ADD)
-                nc.sync.dma_start(out=out[P * h : P * (h + 1), BANK * b : BANK * (b + 1)], in_=o[:])
+        def store(queue, h, b, o):
+            queue.dma_start(out=out[P * h : P * (h + 1), BANK * b : BANK * (b + 1)], in_=o[:])
+
+        def blocks(tile, base):
+            return [tile[:, base + P * i : base + P * (i + 1)] for i in range(BANK // P)]
 
         z0 = [dense(0, b) for b in range(T // BANK)]
         z1 = [dense(1, b) for b in range(T // BANK)]
+        zs = [keep.tile([P, BANK], F32, name="zs%d" % b) for b in range(T // BANK)]
+        for b in range(T // BANK):
+            nc.scalar.copy(out=zs[b][:], in_=z0[b][:])
+        turned = {}
+        for b in (2, 3):
+            turned[b] = psum.tile([P, BANK], F32, name="turned%d" % b, tag="bank%d" % b)
+            for i, (dst, src) in enumerate(zip(blocks(turned[b], 0), blocks(zs[b], 0))):
+                nc.tensor.matmul(dst, lhsT=src, rhs=ident[:], start=(i == 0), stop=False, is_transpose=True)
+
         for i in range(2):
-            nc.vector.tensor_copy(dp[:].indirect(offsets[:, 16 * i : 16 * (i + 1)]), d0[i][:])
-        finish(0, z0)
-        nc.vector.tensor_copy(dp[:].indirect(offsets[:]), d1[:])
-        finish(1, z1)
+            nc.vector.tensor_copy(dp[0][:].indirect(offsets[:, 16 * i : 16 * (i + 1)]), d0[i][:])
+        nc.vector.tensor_copy(dp[1][:].indirect(offsets[:]), d1[:])
+
+        o0 = [keep.tile([P, BANK], F32, name="o0_%d" % b) for b in range(T // BANK)]
+        sums = {}
+        for b in (2, 3):
+            for i, (dst, src) in enumerate(zip(blocks(turned[b], 0), blocks(dp[0], BANK * b))):
+                nc.tensor.matmul(dst, lhsT=src, rhs=ident[:], start=False, stop=(i == 3), is_transpose=True)
+            sums[b] = keep.tile([P, BANK], F32, name="sums%d" % b)
+            nc.scalar.copy(out=sums[b][:], in_=turned[b][:])
+        for b in (0, 1):
+            nc.gpsimd.tensor_tensor(o0[b][:], zs[b][:], dp[0][:, BANK * b : BANK * (b + 1)], ADD)
+            store(nc.scalar, 0, b, o0[b])
+            back = psum.tile([P, BANK], F32, name="back%d" % b, tag="bank%d" % b)
+            for dst, src in zip(blocks(back, 0), blocks(sums[b + 2], 0)):
+                nc.tensor.transpose(dst, src, ident[:])
+            nc.scalar.copy(out=o0[b + 2][:], in_=back[:])
+            store(nc.scalar, 0, b + 2, o0[b + 2])
+
+        for b in range(T // BANK):
+            o = keep.tile([P, BANK], F32, name="o1_%d" % b)
+            nc.vector.tensor_tensor(o[:], z1[b][:], dp[1][:, BANK * b : BANK * (b + 1)], ADD)
+            store(nc.sync, 1, b, o)

@@ -23,6 +23,8 @@ PACK = 4
 CH = 128
 NCH = J // CH
 BANK = 512
+ADDED = (slice(896, 1408), slice(1408, 2048))
+TURNED = (slice(0, 512), slice(512, 896))
 
 
 def load_scales(queue, plane, rows):
@@ -142,44 +144,52 @@ def tile_list_error_feedback_lists_kernel(tc, xq_words, xq_scales, w_words, w_sc
             )
             return z
 
-        def store(queue, h, b, o):
-            queue.dma_start(out=out[P * h : P * (h + 1), BANK * b : BANK * (b + 1)], in_=o[:])
+        def store(h, cols, src):
+            nc.sync.dma_start(out=out[P * h : P * (h + 1), cols], in_=src)
 
-        def blocks(tile, base):
-            return [tile[:, base + P * i : base + P * (i + 1)] for i in range(BANK // P)]
+        def blocks(tile, cols):
+            return [tile[:, i : i + P] for i in range(cols.start, cols.stop, P)]
+
+        def width(cols):
+            return cols.stop - cols.start
 
         z0 = [dense(0, b) for b in range(T // BANK)]
         z1 = [dense(1, b) for b in range(T // BANK)]
-        zs = [keep.tile([P, BANK], F32, name="zs%d" % b) for b in range(T // BANK)]
+        stage = keep.tile([P, T + TURNED[1].stop], F32, name="stage", tag="page")
+        zs = stage[:, 0:T]
+        summed = stage[:, T : T + TURNED[1].stop]
         for b in range(T // BANK):
-            nc.scalar.copy(out=zs[b][:], in_=z0[b][:])
-        turned = {}
-        for b in (2, 3):
-            turned[b] = psum.tile([P, BANK], F32, name="turned%d" % b, tag="bank%d" % b)
-            for i, (dst, src) in enumerate(zip(blocks(turned[b], 0), blocks(zs[b], 0))):
-                nc.tensor.matmul(dst, lhsT=src, rhs=ident[:], start=(i == 0), stop=False, is_transpose=True)
+            nc.scalar.copy(out=zs[:, BANK * b : BANK * (b + 1)], in_=z0[b][:])
+        turned = []
+        for i, cols in enumerate(TURNED):
+            acc = psum.tile([P, width(cols)], F32, name="turned%d" % i, tag="bank%d" % i)
+            turned.append(acc)
+            for n, src in enumerate(blocks(zs, cols)):
+                nc.tensor.matmul(acc[:, P * n : P * (n + 1)], lhsT=src, rhs=ident[:], start=(n == 0), stop=False, is_transpose=True)
 
         for i in range(2):
             nc.vector.tensor_copy(dp[0][:].indirect(offsets[:, 16 * i : 16 * (i + 1)]), d0[i][:])
         nc.vector.tensor_copy(dp[1][:].indirect(offsets[:]), d1[:])
 
-        o0 = [keep.tile([P, BANK], F32, name="o0_%d" % b) for b in range(T // BANK)]
-        sums = {}
-        for b in (2, 3):
-            for i, (dst, src) in enumerate(zip(blocks(turned[b], 0), blocks(dp[0], BANK * b))):
-                nc.tensor.matmul(dst, lhsT=src, rhs=ident[:], start=False, stop=(i == 3), is_transpose=True)
-            sums[b] = keep.tile([P, BANK], F32, name="sums%d" % b)
-            nc.scalar.copy(out=sums[b][:], in_=turned[b][:])
-        for b in (0, 1):
-            nc.gpsimd.tensor_tensor(o0[b][:], zs[b][:], dp[0][:, BANK * b : BANK * (b + 1)], ADD)
-            store(nc.scalar, 0, b, o0[b])
-            back = psum.tile([P, BANK], F32, name="back%d" % b, tag="bank%d" % b)
-            for dst, src in zip(blocks(back, 0), blocks(sums[b + 2], 0)):
-                nc.tensor.transpose(dst, src, ident[:])
-            nc.scalar.copy(out=o0[b + 2][:], in_=back[:])
-            store(nc.scalar, 0, b + 2, o0[b + 2])
+        for i, cols in enumerate(TURNED):
+            for n, src in enumerate(blocks(dp[0], cols)):
+                nc.tensor.matmul(turned[i][:, P * n : P * (n + 1)], lhsT=src, rhs=ident[:], start=False, stop=(n == width(cols) // P - 1), is_transpose=True)
+            nc.scalar.copy(out=summed[:, cols], in_=turned[i][:])
 
+        for i, cols in enumerate(TURNED):
+            gcols = ADDED[i]
+            og = keep.tile([P, width(gcols)], F32, name="og%d" % i)
+            nc.gpsimd.tensor_tensor(og[:], zs[:, gcols], dp[0][:, gcols], ADD)
+            store(0, gcols, og[:])
+            back = psum.tile([P, width(cols)], F32, name="back%d" % i, tag="bank%d" % (2 + i))
+            for n, src in enumerate(blocks(summed, cols)):
+                nc.tensor.transpose(back[:, P * n : P * (n + 1)], src, ident[:])
+            ot = keep.tile([P, width(cols)], F32, name="ot%d" % i)
+            nc.scalar.copy(out=ot[:], in_=back[:])
+            store(0, cols, ot[:])
+
+        o1 = keep.tile([P, T], F32, name="o1", tag="page")
         for b in range(T // BANK):
-            o = keep.tile([P, BANK], F32, name="o1_%d" % b)
-            nc.vector.tensor_tensor(o[:], z1[b][:], dp[1][:, BANK * b : BANK * (b + 1)], ADD)
-            store(nc.sync, 1, b, o)
+            cols = slice(BANK * b, BANK * (b + 1))
+            nc.vector.tensor_tensor(o1[:, cols], z1[b][:], dp[1][:, cols], ADD)
+            store(1, cols, o1[:, cols])

@@ -19,17 +19,32 @@ ADD = mybir.AluOpType.add
 TANH = mybir.ActivationFunctionType.Tanh
 
 P = 128
-PACK = 4
-CH = 128
-NCH = J // CH
+PLANES = 4
+GROUP = 16
+CHUNK = 128
+CHUNKS = J // CHUNK
 BANK = 512
-ADDED = (slice(896, 1408), slice(1408, 2048))
-TURNED = (slice(0, 512), slice(512, 896))
+BANKS_OF_HALF = T // BANK
+
+BY_TRANSPOSES = (slice(0, 384), slice(384, 896))
+BY_GPSIMD = (slice(896, 1536), slice(1536, 2048))
 
 
-def load_scales(queue, plane, rows):
+def width(cols):
+    return cols.stop - cols.start
+
+
+def blocks(ap, cols):
+    return [ap[:, c : c + P] for c in range(cols.start, cols.stop, P)]
+
+
+def entries(offsets, first, count):
+    return offsets[:, first // GROUP : (first + count) // GROUP]
+
+
+def load_scales(queue, scale_tile, rows):
     for q in range(4):
-        queue.dma_start(out=plane[32 * q : 32 * q + 4, :].bitcast(I32), in_=rows[0, 4 * q : 4 * q + 4, :].bitcast(I32))
+        queue.dma_start(out=scale_tile[32 * q : 32 * q + 4, :].bitcast(I32), in_=rows[0, 4 * q : 4 * q + 4, :].bitcast(I32))
 
 
 def tile_list_error_feedback_lists_kernel(tc, xq_words, xq_scales, w_words, w_scales, xf, xc, we_words, we_scales, offs, out):
@@ -38,158 +53,155 @@ def tile_list_error_feedback_lists_kernel(tc, xq_words, xq_scales, w_words, w_sc
         keep = ctx.enter_context(tc.tile_pool(name="keep", bufs=1))
         psum = ctx.enter_context(tc.psum_pool(name="psum", bufs=1))
 
-        offsets = keep.tile([P, J // 16], U16, name="offsets")
-
-        xc_rows = xc.rearrange("(p t) c -> p (t c)", t=PACK)
-        xf_rows = xf.rearrange("(p t) c -> p (t c)", t=PACK)
+        offsets = keep.tile([P, J // GROUP], U16, name="offsets")
+        xc_rows = xc.rearrange("(p r) t -> p (r t)", r=PLANES)
+        xf_rows = xf.rearrange("(p r) t -> p (r t)", r=PLANES)
         xc01 = keep.tile([P, 2 * T], F32, name="xc01")
         xc2 = keep.tile([P, T], F32, name="xc2")
         xc3 = keep.tile([P, T], F32, name="xc3")
-        xf_t = [keep.tile([P, T], F32, name="xf%d" % t) for t in range(PACK)]
+        xf_planes = [keep.tile([P, T], F32, name="xf%d" % r) for r in range(PLANES)]
         nc.sync.dma_start(out=xc01[:], in_=xc_rows[:, 0 : 2 * T])
         nc.sync.dma_start(offsets[:], offs)
-        nc.sync.dma_start(out=xf_t[0][:], in_=xf_rows[:, 0:T])
-        nc.sync.dma_start(out=xf_t[1][:], in_=xf_rows[:, T : 2 * T])
+        nc.sync.dma_start(out=xf_planes[0][:], in_=xf_rows[:, 0:T])
+        nc.sync.dma_start(out=xf_planes[1][:], in_=xf_rows[:, T : 2 * T])
         nc.sync.dma_start(out=xc2[:], in_=xc_rows[:, 2 * T : 3 * T])
-        nc.sync.dma_start(out=xf_t[2][:], in_=xf_rows[:, 2 * T : 3 * T])
+        nc.sync.dma_start(out=xf_planes[2][:], in_=xf_rows[:, 2 * T : 3 * T])
         nc.sync.dma_start(out=xc3[:], in_=xc_rows[:, 3 * T : 4 * T])
-        nc.sync.dma_start(out=xf_t[3][:], in_=xf_rows[:, 3 * T : 4 * T])
-        xc_win = [xc01[:, 0:T], xc01[:, T : 2 * T], xc2[:], xc3[:]]
+        nc.sync.dma_start(out=xf_planes[3][:], in_=xf_rows[:, 3 * T : 4 * T])
+        xc_planes = [xc01[:, 0:T], xc01[:, T : 2 * T], xc2[:], xc3[:]]
 
-        we_sc = keep.tile([P, N], U8, name="we_sc", align_bytes=64)
-        w_sc = keep.tile([P, N], U8, name="w_sc", align_bytes=64)
-        xq_sc = keep.tile([P, T], U8, name="xq_sc", align_bytes=64)
-        for plane in (we_sc, w_sc, xq_sc):
-            nc.vector.memset(plane[:].bitcast(I32), 0)
+        we_scale = keep.tile([P, N], U8, name="we_scale", align_bytes=64)
+        w_scale = keep.tile([P, N], U8, name="w_scale", align_bytes=64)
+        xq_scale = keep.tile([P, T], U8, name="xq_scale", align_bytes=64)
+        for scale_tile in (we_scale, w_scale, xq_scale):
+            nc.vector.memset(scale_tile[:].bitcast(I32), 0)
         ident = keep.tile([P, P], F32, name="ident")
         make_identity(nc, ident[:])
-        load_scales(nc.gpsimd, we_sc, we_scales)
-        load_scales(nc.gpsimd, w_sc, w_scales)
+        load_scales(nc.gpsimd, we_scale, we_scales)
+        load_scales(nc.gpsimd, w_scale, w_scales)
 
-        we_w = keep.tile([P, 2 * N], U8, name="we_w", align_bytes=64)
-        xq_w = keep.tile([P, 2 * T], U8, name="xq_w", align_bytes=64)
-        w_w = keep.tile([P, N], U32, name="w_w", align_bytes=64)
-        nc.sync.dma_start(out=we_w[:].bitcast(I32), in_=we_words[0].bitcast(I32))
-        nc.sync.dma_start(out=xq_w[:].bitcast(I32), in_=xq_words[0].bitcast(I32))
-        nc.sync.dma_start(out=w_w[:].bitcast(I32), in_=w_words[0].rearrange("p n t -> p (n t)").bitcast(I32))
-        load_scales(nc.sync, xq_sc, xq_scales)
+        we_code = keep.tile([P, 2 * N], U8, name="we_code", align_bytes=64)
+        xq_code = keep.tile([P, 2 * T], U8, name="xq_code", align_bytes=64)
+        w_code = keep.tile([P, N], U32, name="w_code", align_bytes=64)
+        nc.sync.dma_start(out=we_code[:].bitcast(I32), in_=we_words[0].bitcast(I32))
+        nc.sync.dma_start(out=xq_code[:].bitcast(I32), in_=xq_words[0].bitcast(I32))
+        nc.sync.dma_start(out=w_code[:].bitcast(I32), in_=w_words[0].rearrange("p n r -> p (n r)").bitcast(I32))
+        load_scales(nc.sync, xq_scale, xq_scales)
 
-        dp = [keep.tile([P, T], F32, name="dp%d" % h) for h in range(2)]
-        for h in range(2):
-            nc.vector.memset(dp[h][:], 0.0)
+        pages = [keep.tile([P, T], F32, name="page%d" % h) for h in range(2)]
+        for page in pages:
+            nc.vector.memset(page[:], 0.0)
 
-        woven = [keep.tile([P, CH, PACK], BF16, name="woven%d" % c, align_bytes=64) for c in range(NCH)]
-        picked = [keep.tile([P, J], F32, name="picked%d" % t) for t in range(PACK)]
-        for t in range(PACK - 1):
-            nc.vector.tensor_copy(picked[t][:], xc_win[t].indirect(offsets[:]))
-            e = keep.tile([P, J], F32, name="e%d" % t)
-            nc.vector.tensor_tensor(e[:], xf_t[t][:].indirect(offsets[:]), picked[t][:], SUB)
-            for c in range(NCH):
-                nc.scalar.copy(out=woven[c][:, :, t], in_=e[:, c * CH : (c + 1) * CH])
-        last = PACK - 1
-        nc.vector.tensor_copy(picked[last][:], xc_win[last].indirect(offsets[:]))
+        woven = [keep.tile([P, CHUNK, PLANES], BF16, name="woven%d" % c, align_bytes=64) for c in range(CHUNKS)]
+        xc_listed = [keep.tile([P, J], F32, name="xc_listed%d" % r) for r in range(PLANES)]
+        last = PLANES - 1
+        for r in range(last):
+            nc.vector.tensor_copy(xc_listed[r][:], xc_planes[r].indirect(offsets[:]))
+            e = keep.tile([P, J], F32, name="e%d" % r)
+            nc.vector.tensor_tensor(e[:], xf_planes[r][:].indirect(offsets[:]), xc_listed[r][:], SUB)
+            for c in range(CHUNKS):
+                nc.scalar.copy(out=woven[c][:, :, r], in_=e[:, c * CHUNK : (c + 1) * CHUNK])
+        nc.vector.tensor_copy(xc_listed[last][:], xc_planes[last].indirect(offsets[:]))
 
-        codes = [keep.tile([P, CH], U32, name="codes%d" % c, align_bytes=64) for c in range(NCH)]
-        scales = [keep.tile([P, CH], U8, name="scales%d" % c, align_bytes=64) for c in range(NCH)]
+        e_code = [keep.tile([P, CHUNK], U32, name="e_code%d" % c, align_bytes=64) for c in range(CHUNKS)]
+        e_scale = [keep.tile([P, CHUNK], U8, name="e_scale%d" % c, align_bytes=64) for c in range(CHUNKS)]
 
-        def gather_last(c):
-            e = keep.tile([P, CH], F32, name="elast%d" % c)
-            cols = slice(c * CH // 16, (c + 1) * CH // 16)
-            nc.vector.tensor_tensor(e[:], xf_t[last][:].indirect(offsets[:, cols]), picked[last][:, c * CH : (c + 1) * CH], SUB)
+        d_first = [keep.tile([P, J // 2], F32, name="d_first%d" % i) for i in range(2)]
+        d_second = keep.tile([P, J], F32, name="d_second")
+
+        def gather_last_plane(c):
+            e = keep.tile([P, CHUNK], F32, name="e_last%d" % c)
+            listed = xf_planes[last][:].indirect(entries(offsets, c * CHUNK, CHUNK))
+            nc.vector.tensor_tensor(e[:], listed, xc_listed[last][:, c * CHUNK : (c + 1) * CHUNK], SUB)
             nc.scalar.copy(out=woven[c][:, :, last], in_=e[:])
 
-        def product(c, h):
-            p = psum.tile([P, CH], F32, name="p%d_%d" % (h, c), tag="bank%d" % (4 * h + c))
+        def listed_product(h, c):
+            acc = psum.tile([P, CHUNK], F32, name="p%d_%d" % (h, c), tag="bank%d" % (CHUNKS * h + c))
             nc.tensor.matmul_mx(
-                out=p[:],
-                lhsT=we_w[:, 2 * P * h : 2 * P * (h + 1)].bitcast(FP4X4),
-                lhsT_scale=we_sc[:, P * h : P * (h + 1)],
-                rhs=codes[c][:].bitcast(FP8X4),
-                rhs_scale=scales[c][:],
+                out=acc[:],
+                lhsT=we_code[:, 2 * P * h : 2 * P * (h + 1)].bitcast(FP4X4),
+                lhsT_scale=we_scale[:, P * h : P * (h + 1)],
+                rhs=e_code[c][:].bitcast(FP8X4),
+                rhs_scale=e_scale[c][:],
                 start=True,
                 stop=True,
             )
-            return p
+            return acc
 
-        def quantise(c):
-            nc.vector.quantize_mx(out=codes[c][:].bitcast(FP8X4), scales=scales[c][:], in_=woven[c][:].rearrange("p j t -> p (j t)"))
-            p0 = product(c, 0)
-            p1.append(product(c, 1))
-            nc.scalar.activation(d0[c // 2][:, (c % 2) * CH : (c % 2 + 1) * CH], p0[:], TANH)
+        def quantise_and_multiply(c):
+            nc.vector.quantize_mx(out=e_code[c][:].bitcast(FP8X4), scales=e_scale[c][:], in_=woven[c][:].rearrange("p j r -> p (j r)"))
+            p_first = listed_product(0, c)
+            p_second = listed_product(1, c)
+            nc.scalar.activation(d_first[c // 2][:, (c % 2) * CHUNK : (c % 2 + 1) * CHUNK], p_first[:], TANH)
+            return p_second
 
-        d0 = [keep.tile([P, 2 * CH], F32, name="d0_%d" % i) for i in range(2)]
-        d1 = keep.tile([P, J], F32, name="d1")
-        p1 = []
-        gather_last(0)
-        gather_last(1)
-        gather_last(2)
-        quantise(0)
-        gather_last(3)
-        quantise(1)
-        quantise(2)
-        quantise(3)
-        for c in range(NCH):
-            nc.scalar.activation(d1[:, c * CH : (c + 1) * CH], p1[c][:], TANH)
+        for c in range(CHUNKS - 1):
+            gather_last_plane(c)
+        seconds = [quantise_and_multiply(0)]
+        gather_last_plane(CHUNKS - 1)
+        for c in range(1, CHUNKS):
+            seconds.append(quantise_and_multiply(c))
+        for c in range(CHUNKS):
+            nc.scalar.activation(d_second[:, c * CHUNK : (c + 1) * CHUNK], seconds[c][:], TANH)
 
-        def dense(h, b):
-            z = psum.tile([P, BANK], F32, name="z%d_%d" % (h, b), tag="bank%d" % (4 * h + b))
+        def dense_product(h, b):
+            acc = psum.tile([P, BANK], F32, name="z%d_%d" % (h, b), tag="bank%d" % (BANKS_OF_HALF * h + b))
             nc.tensor.matmul_mx(
-                out=z[:],
-                lhsT=w_w[:, P * h : P * (h + 1)].bitcast(FP8X4),
-                lhsT_scale=w_sc[:, P * h : P * (h + 1)],
-                rhs=xq_w[:, 2 * BANK * b : 2 * BANK * (b + 1)].bitcast(FP4X4),
-                rhs_scale=xq_sc[:, BANK * b : BANK * (b + 1)],
+                out=acc[:],
+                lhsT=w_code[:, P * h : P * (h + 1)].bitcast(FP8X4),
+                lhsT_scale=w_scale[:, P * h : P * (h + 1)],
+                rhs=xq_code[:, 2 * BANK * b : 2 * BANK * (b + 1)].bitcast(FP4X4),
+                rhs_scale=xq_scale[:, BANK * b : BANK * (b + 1)],
                 start=True,
                 stop=True,
             )
-            return z
+            return acc
 
         def store(h, cols, src):
             nc.sync.dma_start(out=out[P * h : P * (h + 1), cols], in_=src)
 
-        def blocks(tile, cols):
-            return [tile[:, i : i + P] for i in range(cols.start, cols.stop, P)]
+        z_banks = [[dense_product(h, b) for b in range(BANKS_OF_HALF)] for h in range(2)]
 
-        def width(cols):
-            return cols.stop - cols.start
+        staged = keep.tile([P, T + width(BY_TRANSPOSES[1])], F32, name="staged", tag="first_half")
+        z_first = staged[:, 0:T]
+        first_turned_sum = keep.tile([P, width(BY_TRANSPOSES[0])], F32, name="first_turned_sum", tag="by_gpsimd1")
+        turned_sums = [first_turned_sum[:], staged[:, T : T + width(BY_TRANSPOSES[1])]]
+        for b in range(BANKS_OF_HALF):
+            nc.scalar.copy(out=z_first[:, BANK * b : BANK * (b + 1)], in_=z_banks[0][b][:])
 
-        z0 = [dense(0, b) for b in range(T // BANK)]
-        z1 = [dense(1, b) for b in range(T // BANK)]
-        stage = keep.tile([P, T + TURNED[1].stop], F32, name="stage", tag="page")
-        zs = stage[:, 0:T]
-        summed = stage[:, T : T + TURNED[1].stop]
-        for b in range(T // BANK):
-            nc.scalar.copy(out=zs[:, BANK * b : BANK * (b + 1)], in_=z0[b][:])
-        turned = []
-        for i, cols in enumerate(TURNED):
-            acc = psum.tile([P, width(cols)], F32, name="turned%d" % i, tag="bank%d" % i)
-            turned.append(acc)
-            for n, src in enumerate(blocks(zs, cols)):
-                nc.tensor.matmul(acc[:, P * n : P * (n + 1)], lhsT=src, rhs=ident[:], start=(n == 0), stop=False, is_transpose=True)
+        turning = []
+        for i, cols in enumerate(BY_TRANSPOSES):
+            acc = psum.tile([P, width(cols)], F32, name="turning%d" % i, tag="bank%d" % i)
+            turning.append(acc)
+            for m, src in enumerate(blocks(z_first, cols)):
+                nc.tensor.matmul(acc[:, P * m : P * (m + 1)], lhsT=src, rhs=ident[:], start=(m == 0), stop=False, is_transpose=True)
 
         for i in range(2):
-            nc.vector.tensor_copy(dp[0][:].indirect(offsets[:, 16 * i : 16 * (i + 1)]), d0[i][:])
-        nc.vector.tensor_copy(dp[1][:].indirect(offsets[:]), d1[:])
+            nc.vector.tensor_copy(pages[0][:].indirect(entries(offsets, i * J // 2, J // 2)), d_first[i][:])
+        nc.vector.tensor_copy(pages[1][:].indirect(offsets[:]), d_second[:])
 
-        for i, cols in enumerate(TURNED):
-            for n, src in enumerate(blocks(dp[0], cols)):
-                nc.tensor.matmul(turned[i][:, P * n : P * (n + 1)], lhsT=src, rhs=ident[:], start=False, stop=(n == width(cols) // P - 1), is_transpose=True)
-            nc.scalar.copy(out=summed[:, cols], in_=turned[i][:])
+        for i, cols in enumerate(BY_TRANSPOSES):
+            for m, src in enumerate(blocks(pages[0], cols)):
+                closes = m == width(cols) // P - 1
+                nc.tensor.matmul(turning[i][:, P * m : P * (m + 1)], lhsT=src, rhs=ident[:], start=False, stop=closes, is_transpose=True)
+            nc.scalar.copy(out=turned_sums[i], in_=turning[i][:])
 
-        for i, cols in enumerate(TURNED):
-            gcols = ADDED[i]
-            og = keep.tile([P, width(gcols)], F32, name="og%d" % i)
-            nc.gpsimd.tensor_tensor(og[:], zs[:, gcols], dp[0][:, gcols], ADD)
-            store(0, gcols, og[:])
-            back = psum.tile([P, width(cols)], F32, name="back%d" % i, tag="bank%d" % (2 + i))
-            for n, src in enumerate(blocks(summed, cols)):
-                nc.tensor.transpose(back[:, P * n : P * (n + 1)], src, ident[:])
-            ot = keep.tile([P, width(cols)], F32, name="ot%d" % i)
-            nc.scalar.copy(out=ot[:], in_=back[:])
-            store(0, cols, ot[:])
+        for i in range(2):
+            cols = BY_GPSIMD[i]
+            added = keep.tile([P, width(cols)], F32, name="added%d" % i, tag="by_gpsimd%d" % i)
+            nc.gpsimd.tensor_tensor(added[:], z_first[:, cols], pages[0][:, cols], ADD)
+            store(0, cols, added[:])
 
-        o1 = keep.tile([P, T], F32, name="o1", tag="page")
-        for b in range(T // BANK):
+            cols = BY_TRANSPOSES[i]
+            back = psum.tile([P, width(cols)], F32, name="back%d" % i, tag="bank%d" % (len(BY_TRANSPOSES) + i))
+            for m, src in enumerate(blocks(turned_sums[i], slice(0, width(cols)))):
+                nc.tensor.transpose(back[:, P * m : P * (m + 1)], src, ident[:])
+            upright = keep.tile([P, width(cols)], F32, name="upright%d" % i)
+            nc.scalar.copy(out=upright[:], in_=back[:])
+            store(0, cols, upright[:])
+
+        out_second = keep.tile([P, T], F32, name="out_second", tag="first_half")
+        for b in range(BANKS_OF_HALF):
             cols = slice(BANK * b, BANK * (b + 1))
-            nc.vector.tensor_tensor(o1[:, cols], z1[b][:], dp[1][:, cols], ADD)
-            store(1, cols, o1[:, cols])
+            nc.vector.tensor_tensor(out_second[:, cols], z_banks[1][b][:], pages[1][:, cols], ADD)
+            store(1, cols, out_second[:, cols])

from contextlib import ExitStack

import concourse.mybir as mybir
from concourse.masks import make_identity

K, T, J, N = 512, 2048, 512, 256
FLOPS = 2 * K * N * (T + J)

F32 = mybir.dt.float32
BF16 = mybir.dt.bfloat16
I32 = mybir.dt.int32
U32 = mybir.dt.uint32
U16 = mybir.dt.uint16
U8 = mybir.dt.uint8
FP8X4 = mybir.dt.float8_e4m3fn_x4
FP4X4 = mybir.dt.float4_e2m1fn_x4
SUB = mybir.AluOpType.subtract
ADD = mybir.AluOpType.add
TANH = mybir.ActivationFunctionType.Tanh

P = 128
PLANES = 4
GROUP = 16
CHUNK = 128
CHUNKS = J // CHUNK
BANK = 512
BANKS_OF_HALF = T // BANK

BY_TRANSPOSES = (slice(0, 384), slice(384, 896))
BY_GPSIMD = (slice(896, 1536), slice(1536, 2048))


def width(cols):
    return cols.stop - cols.start


def blocks(ap, cols):
    return [ap[:, c : c + P] for c in range(cols.start, cols.stop, P)]


def entries(offsets, first, count):
    return offsets[:, first // GROUP : (first + count) // GROUP]


def load_scales(queue, scale_tile, rows):
    for q in range(4):
        queue.dma_start(out=scale_tile[32 * q : 32 * q + 4, :].bitcast(I32), in_=rows[0, 4 * q : 4 * q + 4, :].bitcast(I32))


def tile_list_error_feedback_lists_kernel(tc, xq_words, xq_scales, w_words, w_scales, xf, xc, we_words, we_scales, offs, out):
    nc = tc.nc
    with ExitStack() as ctx:
        keep = ctx.enter_context(tc.tile_pool(name="keep", bufs=1))
        psum = ctx.enter_context(tc.psum_pool(name="psum", bufs=1))

        offsets = keep.tile([P, J // GROUP], U16, name="offsets")
        xc_rows = xc.rearrange("(p r) t -> p (r t)", r=PLANES)
        xf_rows = xf.rearrange("(p r) t -> p (r t)", r=PLANES)
        xc01 = keep.tile([P, 2 * T], F32, name="xc01")
        xc2 = keep.tile([P, T], F32, name="xc2")
        xc3 = keep.tile([P, T], F32, name="xc3")
        xf_planes = [keep.tile([P, T], F32, name="xf%d" % r) for r in range(PLANES)]
        nc.sync.dma_start(out=xc01[:], in_=xc_rows[:, 0 : 2 * T])
        nc.sync.dma_start(offsets[:], offs)
        nc.sync.dma_start(out=xf_planes[0][:], in_=xf_rows[:, 0:T])
        nc.sync.dma_start(out=xf_planes[1][:], in_=xf_rows[:, T : 2 * T])
        nc.sync.dma_start(out=xc2[:], in_=xc_rows[:, 2 * T : 3 * T])
        nc.sync.dma_start(out=xf_planes[2][:], in_=xf_rows[:, 2 * T : 3 * T])
        nc.sync.dma_start(out=xc3[:], in_=xc_rows[:, 3 * T : 4 * T])
        nc.sync.dma_start(out=xf_planes[3][:], in_=xf_rows[:, 3 * T : 4 * T])
        xc_planes = [xc01[:, 0:T], xc01[:, T : 2 * T], xc2[:], xc3[:]]

        we_scale = keep.tile([P, N], U8, name="we_scale", align_bytes=64)
        w_scale = keep.tile([P, N], U8, name="w_scale", align_bytes=64)
        xq_scale = keep.tile([P, T], U8, name="xq_scale", align_bytes=64)
        for scale_tile in (we_scale, w_scale, xq_scale):
            nc.vector.memset(scale_tile[:].bitcast(I32), 0)
        ident = keep.tile([P, P], F32, name="ident")
        make_identity(nc, ident[:])
        load_scales(nc.gpsimd, we_scale, we_scales)
        load_scales(nc.gpsimd, w_scale, w_scales)

        we_code = keep.tile([P, 2 * N], U8, name="we_code", align_bytes=64)
        xq_code = keep.tile([P, 2 * T], U8, name="xq_code", align_bytes=64)
        w_code = keep.tile([P, N], U32, name="w_code", align_bytes=64)
        nc.sync.dma_start(out=we_code[:].bitcast(I32), in_=we_words[0].bitcast(I32))
        nc.sync.dma_start(out=xq_code[:].bitcast(I32), in_=xq_words[0].bitcast(I32))
        nc.sync.dma_start(out=w_code[:].bitcast(I32), in_=w_words[0].rearrange("p n r -> p (n r)").bitcast(I32))
        load_scales(nc.sync, xq_scale, xq_scales)

        pages = [keep.tile([P, T], F32, name="page%d" % h) for h in range(2)]
        for page in pages:
            nc.vector.memset(page[:], 0.0)

        woven = [keep.tile([P, CHUNK, PLANES], BF16, name="woven%d" % c, align_bytes=64) for c in range(CHUNKS)]
        xc_listed = [keep.tile([P, J], F32, name="xc_listed%d" % r) for r in range(PLANES)]
        last = PLANES - 1
        for r in range(last):
            nc.vector.tensor_copy(xc_listed[r][:], xc_planes[r].indirect(offsets[:]))
            e = keep.tile([P, J], F32, name="e%d" % r)
            nc.vector.tensor_tensor(e[:], xf_planes[r][:].indirect(offsets[:]), xc_listed[r][:], SUB)
            for c in range(CHUNKS):
                nc.scalar.copy(out=woven[c][:, :, r], in_=e[:, c * CHUNK : (c + 1) * CHUNK])
        nc.vector.tensor_copy(xc_listed[last][:], xc_planes[last].indirect(offsets[:]))

        e_code = [keep.tile([P, CHUNK], U32, name="e_code%d" % c, align_bytes=64) for c in range(CHUNKS)]
        e_scale = [keep.tile([P, CHUNK], U8, name="e_scale%d" % c, align_bytes=64) for c in range(CHUNKS)]

        d_first = [keep.tile([P, J // 2], F32, name="d_first%d" % i) for i in range(2)]
        d_second = keep.tile([P, J], F32, name="d_second")

        def gather_last_plane(c):
            e = keep.tile([P, CHUNK], F32, name="e_last%d" % c)
            listed = xf_planes[last][:].indirect(entries(offsets, c * CHUNK, CHUNK))
            nc.vector.tensor_tensor(e[:], listed, xc_listed[last][:, c * CHUNK : (c + 1) * CHUNK], SUB)
            nc.scalar.copy(out=woven[c][:, :, last], in_=e[:])

        def listed_product(h, c):
            acc = psum.tile([P, CHUNK], F32, name="p%d_%d" % (h, c), tag="bank%d" % (CHUNKS * h + c))
            nc.tensor.matmul_mx(
                out=acc[:],
                lhsT=we_code[:, 2 * P * h : 2 * P * (h + 1)].bitcast(FP4X4),
                lhsT_scale=we_scale[:, P * h : P * (h + 1)],
                rhs=e_code[c][:].bitcast(FP8X4),
                rhs_scale=e_scale[c][:],
                start=True,
                stop=True,
            )
            return acc

        def quantise_and_multiply(c):
            nc.vector.quantize_mx(out=e_code[c][:].bitcast(FP8X4), scales=e_scale[c][:], in_=woven[c][:].rearrange("p j r -> p (j r)"))
            p_first = listed_product(0, c)
            p_second = listed_product(1, c)
            nc.scalar.activation(d_first[c // 2][:, (c % 2) * CHUNK : (c % 2 + 1) * CHUNK], p_first[:], TANH)
            return p_second

        for c in range(CHUNKS - 1):
            gather_last_plane(c)
        seconds = [quantise_and_multiply(0)]
        gather_last_plane(CHUNKS - 1)
        for c in range(1, CHUNKS):
            seconds.append(quantise_and_multiply(c))
        for c in range(CHUNKS):
            nc.scalar.activation(d_second[:, c * CHUNK : (c + 1) * CHUNK], seconds[c][:], TANH)

        def dense_product(h, b):
            acc = psum.tile([P, BANK], F32, name="z%d_%d" % (h, b), tag="bank%d" % (BANKS_OF_HALF * h + b))
            nc.tensor.matmul_mx(
                out=acc[:],
                lhsT=w_code[:, P * h : P * (h + 1)].bitcast(FP8X4),
                lhsT_scale=w_scale[:, P * h : P * (h + 1)],
                rhs=xq_code[:, 2 * BANK * b : 2 * BANK * (b + 1)].bitcast(FP4X4),
                rhs_scale=xq_scale[:, BANK * b : BANK * (b + 1)],
                start=True,
                stop=True,
            )
            return acc

        def store(h, cols, src):
            nc.sync.dma_start(out=out[P * h : P * (h + 1), cols], in_=src)

        z_banks = [[dense_product(h, b) for b in range(BANKS_OF_HALF)] for h in range(2)]

        staged = keep.tile([P, T + width(BY_TRANSPOSES[1])], F32, name="staged", tag="first_half")
        z_first = staged[:, 0:T]
        first_turned_sum = keep.tile([P, width(BY_TRANSPOSES[0])], F32, name="first_turned_sum", tag="by_gpsimd1")
        turned_sums = [first_turned_sum[:], staged[:, T : T + width(BY_TRANSPOSES[1])]]
        for b in range(BANKS_OF_HALF):
            nc.scalar.copy(out=z_first[:, BANK * b : BANK * (b + 1)], in_=z_banks[0][b][:])

        turning = []
        for i, cols in enumerate(BY_TRANSPOSES):
            acc = psum.tile([P, width(cols)], F32, name="turning%d" % i, tag="bank%d" % i)
            turning.append(acc)
            for m, src in enumerate(blocks(z_first, cols)):
                nc.tensor.matmul(acc[:, P * m : P * (m + 1)], lhsT=src, rhs=ident[:], start=(m == 0), stop=False, is_transpose=True)

        for i in range(2):
            nc.vector.tensor_copy(pages[0][:].indirect(entries(offsets, i * J // 2, J // 2)), d_first[i][:])
        nc.vector.tensor_copy(pages[1][:].indirect(offsets[:]), d_second[:])

        for i, cols in enumerate(BY_TRANSPOSES):
            for m, src in enumerate(blocks(pages[0], cols)):
                closes = m == width(cols) // P - 1
                nc.tensor.matmul(turning[i][:, P * m : P * (m + 1)], lhsT=src, rhs=ident[:], start=False, stop=closes, is_transpose=True)
            nc.scalar.copy(out=turned_sums[i], in_=turning[i][:])

        for i in range(2):
            cols = BY_GPSIMD[i]
            added = keep.tile([P, width(cols)], F32, name="added%d" % i, tag="by_gpsimd%d" % i)
            nc.gpsimd.tensor_tensor(added[:], z_first[:, cols], pages[0][:, cols], ADD)
            store(0, cols, added[:])

            cols = BY_TRANSPOSES[i]
            back = psum.tile([P, width(cols)], F32, name="back%d" % i, tag="bank%d" % (len(BY_TRANSPOSES) + i))
            for m, src in enumerate(blocks(turned_sums[i], slice(0, width(cols)))):
                nc.tensor.transpose(back[:, P * m : P * (m + 1)], src, ident[:])
            upright = keep.tile([P, width(cols)], F32, name="upright%d" % i)
            nc.scalar.copy(out=upright[:], in_=back[:])
            store(0, cols, upright[:])

        out_second = keep.tile([P, T], F32, name="out_second", tag="first_half")
        for b in range(BANKS_OF_HALF):
            cols = slice(BANK * b, BANK * (b + 1))
            nc.vector.tensor_tensor(out_second[:, cols], z_banks[1][b][:], pages[1][:, cols], ADD)
            store(1, cols, out_second[:, cols])
